import numpy as np
import ml_dtypes


def mxq(x, axis, fmt="e4m3"):
    dtype, down = {"e4m3": (ml_dtypes.float8_e4m3fn, 7), "e5m2": (ml_dtypes.float8_e5m2, 14)}[fmt]
    v = np.moveaxis(np.asarray(x, np.float32).astype(ml_dtypes.bfloat16).astype(np.float64), axis, -1)
    blocks = v.reshape(v.shape[:-1] + (-1, 32))
    amax = np.abs(blocks).max(-1, keepdims=True)
    byte = np.maximum(np.where(amax > 0, np.frexp(amax)[1] - 1 + 127, 0) - down, 1)
    scale = np.exp2(byte - 127.0)
    codes = (blocks / scale).astype(np.float32).astype(dtype).astype(np.float64)
    return np.moveaxis((codes * scale).reshape(v.shape), -1, axis)


WIDE = False


def mx_kscale(k):
    if not WIDE:
        return np.ones(k)
    levels = np.array([10, -10, 5, -5, 0])
    if k % 512:
        return np.exp2(np.random.permutation(np.resize(levels, k // 32))).repeat(32)
    a = np.empty((k // 512, 16))
    for p in range(k // 512):
        a[p, :8] = np.random.permutation(np.resize(levels, 8))
        for g in range(8):
            far = levels[np.abs(levels - a[p, g]) >= 10]
            a[p, g + 8] = far[np.random.randint(len(far))]
    return np.exp2(a.ravel()).repeat(32)


def f64(x):
    return np.asarray(x).astype(np.float64)


def striped(idx):
    return np.tile(np.asarray(idx).reshape(-1, 16).T, (8, 1)).astype(np.uint16)


def unstriped(offs):
    return offs[:16].T.reshape(-1).astype(np.int64)


E2M1 = np.array([0.0, 0.5, 1.0, 1.5, 2.0, 3.0, 4.0, 6.0, -0.0, -0.5, -1.0, -1.5, -2.0, -3.0, -4.0, -6.0])


def pack_weight(w, fmt):
    k, n = w.shape
    w = f64(np.asarray(w, np.float32).astype(ml_dtypes.bfloat16)).reshape(k // 32, 32, n)
    amax = np.abs(w).max(1)
    if fmt == "e4m3":
        byte = np.frexp(amax)[1] - 1 + 127 - 7
    else:
        mant, ex = np.frexp(amax / 6.0)
        byte = np.where(mant > 0.5, ex, ex - 1) + 127
    byte = np.clip(np.where(amax > 0, byte, 1), 1, 254)
    scaled = (w * np.exp2(127.0 - byte)[:, None, :]).reshape(k, n).astype(np.float32)
    by_word = np.ascontiguousarray(scaled.reshape(k // 512, 128, 4, n).transpose(0, 1, 3, 2))
    if fmt == "e4m3":
        words = by_word.astype(ml_dtypes.float8_e4m3fn).view(np.uint8)
    else:
        c = by_word.astype(ml_dtypes.float4_e2m1fn).view(np.uint8) & 0xF
        words = (c[..., 0::2] | (c[..., 1::2] << 4)).reshape(k // 512, 128, 2 * n)
    return np.ascontiguousarray(words), np.ascontiguousarray(byte.astype(np.uint8).reshape(k // 512, 16, n))


def unpack_weight(words, scales, fmt):
    g, _, n = scales.shape
    words = np.ascontiguousarray(words).reshape(g, 128, n, -1)
    if fmt == "e4m3":
        vals = words.view(ml_dtypes.float8_e4m3fn).astype(np.float64)
    else:
        nib = np.empty((g, 128, n, 4), np.uint8)
        nib[..., 0::2] = words & 0xF
        nib[..., 1::2] = words >> 4
        vals = E2M1[nib]
    vals = vals * np.repeat(np.exp2(scales.astype(np.float64) - 127.0), 8, axis=1)[..., None]
    return vals.transpose(0, 1, 3, 2).reshape(g * 512, n)


def softplus(v):
    return np.log(1.0 + np.exp(v))


K, L, T, C, J = 1024, 512, 256, 1024, 512


def setup_inputs():
    n = np.random.standard_normal
    idx = np.random.permutation(C)[:J]
    fk = mx_kscale(K)
    fl = mx_kscale(L)
    wcp = pack_weight(n((K, C)) * 1 / np.sqrt(K) * fk[:, None], "e2m1")
    xsp = pack_weight(n((L, T)) / fl[:, None], "e4m3")
    wsp = pack_weight(n((L, J)) * 1 / np.sqrt(L) * fl[:, None], "e2m1")
    return {
        "xt": (n((K, T)) / fk[:, None]).astype(np.float32),
        "wc_words": wcp[0],
        "wc_scales": wcp[1],
        "xs_words": xsp[0],
        "xs_scales": xsp[1],
        "ws_words": wsp[0],
        "ws_scales": wsp[1],
        "offs": striped(idx),
    }


def reference(xt, wc_words, wc_scales, xs_words, xs_scales, ws_words, ws_scales, offs):
    idx = unstriped(offs)
    wcu = unpack_weight(wc_words, wc_scales, "e2m1")
    xsu = unpack_weight(xs_words, xs_scales, "e4m3")
    wsu = unpack_weight(ws_words, ws_scales, "e2m1")
    xtq = mxq(f64(xt), 0, "e4m3")
    z = xtq.T @ wcu
    s = xsu.T @ wsu
    y = softplus(np.max(z, axis=1, keepdims=True) - z[:, idx]) - 0.5 * s
    return y

@@ -1,0 +1,147 @@
+from contextlib import ExitStack
+
+import concourse.mybir as mybir
+
+K, L, T, C, J = 1024, 512, 256, 1024, 512
+FLOPS = 2 * K * T * C + 2 * L * T * J
+
+F32 = mybir.dt.float32
+BF16 = mybir.dt.bfloat16
+I32 = mybir.dt.int32
+U32 = mybir.dt.uint32
+U16 = mybir.dt.uint16
+U8 = mybir.dt.uint8
+FP8X4 = mybir.dt.float8_e4m3fn_x4
+FP4X4 = mybir.dt.float4_e2m1fn_x4
+ALU = mybir.AluOpType
+ACT = mybir.ActivationFunctionType
+
+P = 128
+PACK = 4
+PASSES = K // (P * PACK)
+TILES = T // P
+BANK = 512
+HALVES = C // BANK
+GATHER_CUTS = ((0, J), (0, 320, J))
+OUT_CUTS = (0, 128, 320, J)
+
+
+def tile_list_runner_up_gap_kernel(tc, xt, wc_words, wc_scales, xs_words, xs_scales, ws_words, ws_scales, offs, out):
+    nc = tc.nc
+    with ExitStack() as ctx:
+        keep = ctx.enter_context(tc.tile_pool(name="keep", bufs=1))
+        psum = ctx.enter_context(tc.psum_pool(name="psum", bufs=1))
+
+        offsets = keep.tile([P, J // 16], U16, name="offsets")
+        x_raw = [[keep.tile([P, PACK, P], F32, name=f"x_raw{i}{a}") for a in range(PASSES)] for i in range(TILES)]
+        wc_w = [keep.tile([P, 2 * C], U8, name=f"wc_w{a}", align_bytes=64) for a in range(PASSES)]
+        wc_s = keep.tile([P, PASSES * C], U8, name="wc_s", align_bytes=64)
+        xs_w = keep.tile([P, 4 * T], U8, name="xs_w", align_bytes=64)
+        ws_w = keep.tile([P, 2 * J], U8, name="ws_w", align_bytes=64)
+        xs_s = keep.tile([P, T], U8, name="xs_s", align_bytes=64)
+        ws_s = keep.tile([P, J], U8, name="ws_s", align_bytes=64)
+
+        nc.vector.memset(wc_s[:].bitcast(I32), 0)
+        nc.vector.memset(xs_s[:].bitcast(I32), 0)
+        nc.vector.memset(ws_s[:].bitcast(I32), 0)
+
+        def load_x(queue, i, a):
+            rows = xt[a * P * PACK : (a + 1) * P * PACK, i * P : (i + 1) * P]
+            queue.dma_start(out=x_raw[i][a][:], in_=rows.rearrange("(p j) t -> p j t", j=PACK))
+
+        def load_wc(queue, a):
+            queue.dma_start(out=wc_w[a][:].bitcast(I32), in_=wc_words[a].bitcast(I32))
+
+        load_x(nc.sync, 0, 0)
+        for q in range(4):
+            nc.sync.dma_start(
+                out=wc_s[32 * q : 32 * q + 4, :].bitcast(I32).rearrange("r (z c) -> r z c", z=PASSES),
+                in_=wc_scales.bitcast(I32)[:, 4 * q : 4 * q + 4, :].rearrange("z r c -> r z c"),
+            )
+        load_wc(nc.sync, 0)
+        load_x(nc.sync, 0, 1)
+        load_wc(nc.sync, 1)
+        load_x(nc.sync, 1, 0)
+        load_x(nc.sync, 1, 1)
+        nc.sync.dma_start(offsets[:], offs)
+        nc.sync.dma_start(out=xs_w[:].bitcast(I32), in_=xs_words[0].rearrange("p t r -> p (t r)").bitcast(I32))
+        nc.sync.dma_start(out=ws_w[:].bitcast(I32), in_=ws_words[0].bitcast(I32))
+        for q in range(4):
+            nc.sync.dma_start(out=xs_s[32 * q : 32 * q + 4, :].bitcast(I32), in_=xs_scales[0].bitcast(I32)[4 * q : 4 * q + 4, :])
+            nc.sync.dma_start(out=ws_s[32 * q : 32 * q + 4, :].bitcast(I32), in_=ws_scales[0].bitcast(I32)[4 * q : 4 * q + 4, :])
+
+        z_ps = [[psum.tile([P, BANK], F32, name=f"z_ps{i}{h}", tag=f"bank{i}{h}") for h in range(HALVES)] for i in range(TILES)]
+
+        for i in range(TILES):
+            codes, scales = [], []
+            for a in range(PASSES):
+                x_bf = keep.tile([P, P, PACK], BF16, name=f"x_bf{i}{a}", tag=f"x_bf{i}{a}", align_bytes=64)
+                src = x_raw[i][a][:].rearrange("p j (c e) -> p c j e", e=4)
+                dst = x_bf[:].rearrange("p (c e) j -> p c j e", e=4)
+                if i == 0:
+                    nc.vector.tensor_copy(out=dst, in_=src)
+                else:
+                    nc.scalar.copy(out=dst, in_=src)
+                x_q = keep.tile([P, P], U32, name=f"x_q{i}{a}", align_bytes=64)
+                x_s = keep.tile([P, P], U8, name=f"x_s{i}{a}", align_bytes=64)
+                nc.vector.quantize_mx(out=x_q[:].bitcast(FP8X4), scales=x_s[:], in_=x_bf[:].rearrange("p c j -> p (c j)"))
+                codes.append(x_q)
+                scales.append(x_s)
+            for a in range(PASSES):
+                for h in range(HALVES):
+                    nc.tensor.matmul_mx(
+                        out=z_ps[i][h][:],
+                        lhsT=codes[a][:].bitcast(FP8X4),
+                        lhsT_scale=scales[a][:],
+                        rhs=wc_w[a][:, 2 * BANK * h : 2 * BANK * (h + 1)].bitcast(FP4X4),
+                        rhs_scale=wc_s[:, a * C + BANK * h : a * C + BANK * (h + 1)],
+                        start=(a == 0),
+                        stop=(a == PASSES - 1),
+                    )
+
+        best = []
+        picked = [keep.tile([P, J], F32, name=f"picked{i}", tag=f"x_bf{TILES - 1}{PASSES - 1 - i}", align_bytes=64) for i in range(TILES)]
+        decay = keep.tile([P, TILES, J], F32, name="decay")
+        for i in range(TILES):
+            z = keep.tile([P, C], F32, name=f"z{i}", tag=f"z{i}")
+            first = keep.tile([P, 1], F32, name=f"first{i}")
+            best_i = keep.tile([P, 1], F32, name=f"best{i}")
+            minus_best = keep.tile([P, 1], F32, name=f"minus_best{i}")
+            nc.vector.tensor_scalar(out=z[:, 0:BANK], in0=z_ps[i][0][:], scalar1=1.0, scalar2=None, op0=ALU.mult, op1=ALU.max, accum_out=first[:])
+            nc.vector.tensor_scalar(out=z[:, BANK:C], in0=z_ps[i][1][:], scalar1=1.0, scalar2=first[:], op0=ALU.mult, op1=ALU.max, accum_out=best_i[:])
+            nc.scalar.mul(minus_best[:], best_i[:], -1.0)
+            cuts = GATHER_CUTS[i]
+            for j0, j1 in zip(cuts[:-1], cuts[1:]):
+                nc.vector.tensor_copy(picked[i][:, j0:j1], z[:].indirect(offsets[:, j0 // 16 : j1 // 16]))
+                nc.scalar.activation(out=decay[:, i, j0:j1], in_=picked[i][:, j0:j1], func=ACT.Exp, bias=minus_best[:])
+            best.append(best_i)
+
+        s_ps = [psum.tile([P, J], F32, name=f"s_ps{i}", tag=f"bank{TILES - 1}{i}") for i in range(TILES)]
+        for i in range(TILES):
+            nc.tensor.matmul_mx(
+                out=s_ps[i][:],
+                lhsT=xs_w[:, 4 * P * i : 4 * P * (i + 1)].bitcast(FP8X4),
+                lhsT_scale=xs_s[:, P * i : P * (i + 1)],
+                rhs=ws_w[:].bitcast(FP4X4),
+                rhs_scale=ws_s[:],
+                start=True,
+                stop=True,
+            )
+
+        gaps = []
+        both = keep.tile([P, TILES, J], F32, name="both", tag=f"z{TILES - 1}")
+        rest = keep.tile([P, TILES, J], F32, name="rest")
+        for i in range(TILES):
+            gap = both[:, i, :]
+            nc.vector.tensor_scalar(out=gap, in0=picked[i][:], scalar1=-1.0, scalar2=best[i][:], op0=ALU.mult, op1=ALU.add)
+            gaps.append(gap)
+        for i in range(TILES):
+            nc.vector.scalar_tensor_tensor(out=rest[:, i, :], in0=s_ps[i][:], scalar=-0.5, in1=gaps[i], op0=ALU.mult, op1=ALU.add)
+
+        out_rows = out.rearrange("(i p) j -> p i j", p=P)
+        for j0, j1 in reversed(list(zip(OUT_CUTS[:-1], OUT_CUTS[1:]))):
+            soft = keep.tile([P, TILES, j1 - j0], F32, name=f"soft{j0}")
+            nc.scalar.activation(out=soft[:], in_=decay[:, :, j0:j1], func=ACT.Ln, bias=1.0)
+            y = keep.tile([P, TILES, j1 - j0], F32, name=f"y{j0}")
+            nc.vector.tensor_tensor(out=y[:], in0=rest[:, :, j0:j1], in1=soft[:], op=ALU.add)
+            nc.sync.dma_start(out=out_rows[:, :, j0:j1], in_=y[:])

@@ -18,12 +18,9 @@ ACT = mybir.ActivationFunctionType
 
 P = 128
 PACK = 4
-PASSES = K // (P * PACK)
-TILES = T // P
 BANK = 512
-HALVES = C // BANK
-GATHER_CUTS = ((0, J), (0, 320, J))
-OUT_CUTS = (0, 128, 320, J)
+VECTOR_COLS = 80
+OUT_COLS = 128
 
 
 def tile_list_runner_up_gap_kernel(tc, xt, wc_words, wc_scales, xs_words, xs_scales, ws_words, ws_scales, offs, out):
@@ -33,9 +30,10 @@ def tile_list_runner_up_gap_kernel(tc, xt, wc_words, wc_scales, xs_words, xs_sca
         psum = ctx.enter_context(tc.psum_pool(name="psum", bufs=1))
 
         offsets = keep.tile([P, J // 16], U16, name="offsets")
-        x_raw = [[keep.tile([P, PACK, P], F32, name=f"x_raw{i}{a}") for a in range(PASSES)] for i in range(TILES)]
-        wc_w = [keep.tile([P, 2 * C], U8, name=f"wc_w{a}", align_bytes=64) for a in range(PASSES)]
-        wc_s = keep.tile([P, PASSES * C], U8, name="wc_s", align_bytes=64)
+        x_raw = [[keep.tile([P, PACK, P], F32, name=f"x_raw{i}{a}", tag=f"x_raw{i}{a}") for a in range(2)] for i in range(2)]
+        wc_first = keep.tile([P, 2 * C], U8, name="wc_first", align_bytes=64)
+        wc_last = [keep.tile([P, 2 * BANK], U8, name=f"wc_last{h}", tag=f"wc_last{h}", align_bytes=64) for h in range(2)]
+        wc_s = keep.tile([P, 2 * C], U8, name="wc_s", align_bytes=64)
         xs_w = keep.tile([P, 4 * T], U8, name="xs_w", align_bytes=64)
         ws_w = keep.tile([P, 2 * J], U8, name="ws_w", align_bytes=64)
         xs_s = keep.tile([P, T], U8, name="xs_s", align_bytes=64)
@@ -45,24 +43,22 @@ def tile_list_runner_up_gap_kernel(tc, xt, wc_words, wc_scales, xs_words, xs_sca
         nc.vector.memset(xs_s[:].bitcast(I32), 0)
         nc.vector.memset(ws_s[:].bitcast(I32), 0)
 
-        def load_x(queue, i, a):
+        def load_x(i, a):
             rows = xt[a * P * PACK : (a + 1) * P * PACK, i * P : (i + 1) * P]
-            queue.dma_start(out=x_raw[i][a][:], in_=rows.rearrange("(p j) t -> p j t", j=PACK))
+            nc.sync.dma_start(out=x_raw[i][a][:], in_=rows.rearrange("(p j) t -> p j t", j=PACK))
 
-        def load_wc(queue, a):
-            queue.dma_start(out=wc_w[a][:].bitcast(I32), in_=wc_words[a].bitcast(I32))
-
-        load_x(nc.sync, 0, 0)
+        load_x(0, 0)
+        nc.sync.dma_start(out=wc_first[:].bitcast(I32), in_=wc_words[0].bitcast(I32))
         for q in range(4):
             nc.sync.dma_start(
-                out=wc_s[32 * q : 32 * q + 4, :].bitcast(I32).rearrange("r (z c) -> r z c", z=PASSES),
+                out=wc_s[32 * q : 32 * q + 4, :].bitcast(I32).rearrange("r (z c) -> r z c", z=2),
                 in_=wc_scales.bitcast(I32)[:, 4 * q : 4 * q + 4, :].rearrange("z r c -> r z c"),
             )
-        load_wc(nc.sync, 0)
-        load_x(nc.sync, 0, 1)
-        load_wc(nc.sync, 1)
-        load_x(nc.sync, 1, 0)
-        load_x(nc.sync, 1, 1)
+        load_x(0, 1)
+        for h in range(2):
+            nc.sync.dma_start(out=wc_last[h][:].bitcast(I32), in_=wc_words[1].bitcast(I32)[:, h * BANK // 2 : (h + 1) * BANK // 2])
+        load_x(1, 0)
+        load_x(1, 1)
         nc.sync.dma_start(offsets[:], offs)
         nc.sync.dma_start(out=xs_w[:].bitcast(I32), in_=xs_words[0].rearrange("p t r -> p (t r)").bitcast(I32))
         nc.sync.dma_start(out=ws_w[:].bitcast(I32), in_=ws_words[0].bitcast(I32))
@@ -70,54 +66,85 @@ def tile_list_runner_up_gap_kernel(tc, xt, wc_words, wc_scales, xs_words, xs_sca
             nc.sync.dma_start(out=xs_s[32 * q : 32 * q + 4, :].bitcast(I32), in_=xs_scales[0].bitcast(I32)[4 * q : 4 * q + 4, :])
             nc.sync.dma_start(out=ws_s[32 * q : 32 * q + 4, :].bitcast(I32), in_=ws_scales[0].bitcast(I32)[4 * q : 4 * q + 4, :])
 
-        z_ps = [[psum.tile([P, BANK], F32, name=f"z_ps{i}{h}", tag=f"bank{i}{h}") for h in range(HALVES)] for i in range(TILES)]
+        z_ps = [[psum.tile([P, BANK], F32, name=f"z_ps{i}{h}", tag=f"bank{i}{h}") for h in range(2)] for i in range(2)]
+        z = [keep.tile([P, C], F32, name=f"z{i}", tag=f"z{i}") for i in range(2)]
+        half_best = [[keep.tile([P, 1], F32, name=f"half_best{i}{h}") for h in range(2)] for i in range(2)]
+        minus_best = [keep.tile([P, 1], F32, name=f"minus_best{i}") for i in range(2)]
+        decay = keep.tile([P, 2, J], F32, name="decay")
+        below = [keep.tile([P, J], F32, name=f"below{i}") for i in range(2)]
+        x_bf = {}
 
-        for i in range(TILES):
-            codes, scales = [], []
-            for a in range(PASSES):
-                x_bf = keep.tile([P, P, PACK], BF16, name=f"x_bf{i}{a}", tag=f"x_bf{i}{a}", align_bytes=64)
-                src = x_raw[i][a][:].rearrange("p j (c e) -> p c j e", e=4)
-                dst = x_bf[:].rearrange("p (c e) j -> p c j e", e=4)
-                if i == 0:
-                    nc.vector.tensor_copy(out=dst, in_=src)
-                else:
-                    nc.scalar.copy(out=dst, in_=src)
-                x_q = keep.tile([P, P], U32, name=f"x_q{i}{a}", align_bytes=64)
-                x_s = keep.tile([P, P], U8, name=f"x_s{i}{a}", align_bytes=64)
-                nc.vector.quantize_mx(out=x_q[:].bitcast(FP8X4), scales=x_s[:], in_=x_bf[:].rearrange("p c j -> p (c j)"))
-                codes.append(x_q)
-                scales.append(x_s)
-            for a in range(PASSES):
-                for h in range(HALVES):
-                    nc.tensor.matmul_mx(
-                        out=z_ps[i][h][:],
-                        lhsT=codes[a][:].bitcast(FP8X4),
-                        lhsT_scale=scales[a][:],
-                        rhs=wc_w[a][:, 2 * BANK * h : 2 * BANK * (h + 1)].bitcast(FP4X4),
-                        rhs_scale=wc_s[:, a * C + BANK * h : a * C + BANK * (h + 1)],
-                        start=(a == 0),
-                        stop=(a == PASSES - 1),
-                    )
+        def round_x(i, a, vector_cols):
+            x_bf[i, a] = keep.tile([P, P, PACK], BF16, name=f"x_bf{i}{a}", align_bytes=64)
+            src = x_raw[i][a][:].rearrange("p j (c e) -> p c j e", e=4)
+            dst = x_bf[i, a][:].rearrange("p (c e) j -> p c j e", e=4)
+            cut = vector_cols // 4
+            if cut > 0:
+                nc.vector.tensor_copy(out=dst[:, :cut], in_=src[:, :cut])
+            nc.scalar.copy(out=dst[:, cut:], in_=src[:, cut:])
 
-        best = []
-        picked = [keep.tile([P, J], F32, name=f"picked{i}", tag=f"x_bf{TILES - 1}{PASSES - 1 - i}", align_bytes=64) for i in range(TILES)]
-        decay = keep.tile([P, TILES, J], F32, name="decay")
-        for i in range(TILES):
-            z = keep.tile([P, C], F32, name=f"z{i}", tag=f"z{i}")
-            first = keep.tile([P, 1], F32, name=f"first{i}")
-            best_i = keep.tile([P, 1], F32, name=f"best{i}")
-            minus_best = keep.tile([P, 1], F32, name=f"minus_best{i}")
-            nc.vector.tensor_scalar(out=z[:, 0:BANK], in0=z_ps[i][0][:], scalar1=1.0, scalar2=None, op0=ALU.mult, op1=ALU.max, accum_out=first[:])
-            nc.vector.tensor_scalar(out=z[:, BANK:C], in0=z_ps[i][1][:], scalar1=1.0, scalar2=first[:], op0=ALU.mult, op1=ALU.max, accum_out=best_i[:])
-            nc.scalar.mul(minus_best[:], best_i[:], -1.0)
-            cuts = GATHER_CUTS[i]
-            for j0, j1 in zip(cuts[:-1], cuts[1:]):
-                nc.vector.tensor_copy(picked[i][:, j0:j1], z[:].indirect(offsets[:, j0 // 16 : j1 // 16]))
-                nc.scalar.activation(out=decay[:, i, j0:j1], in_=picked[i][:, j0:j1], func=ACT.Exp, bias=minus_best[:])
-            best.append(best_i)
+        def product_pass(i, a):
+            x_q = keep.tile([P, P], U32, name=f"x_q{i}{a}", align_bytes=64)
+            x_s = keep.tile([P, P], U8, name=f"x_s{i}{a}", align_bytes=64)
+            nc.vector.quantize_mx(out=x_q[:].bitcast(FP8X4), scales=x_s[:], in_=x_bf[i, a][:].rearrange("p c j -> p (c j)"))
+            for h in range(2):
+                words = wc_first[:, 2 * BANK * h : 2 * BANK * (h + 1)] if a == 0 else wc_last[h][:]
+                nc.tensor.matmul_mx(
+                    out=z_ps[i][h][:],
+                    lhsT=x_q[:].bitcast(FP8X4),
+                    lhsT_scale=x_s[:],
+                    rhs=words.bitcast(FP4X4),
+                    rhs_scale=wc_s[:, a * C + BANK * h : a * C + BANK * (h + 1)],
+                    start=(a == 0),
+                    stop=(a == 1),
+                )
 
-        s_ps = [psum.tile([P, J], F32, name=f"s_ps{i}", tag=f"bank{TILES - 1}{i}") for i in range(TILES)]
-        for i in range(TILES):
+        def empty_bank(i, h):
+            nc.vector.tensor_scalar(
+                out=z[i][:, BANK * h : BANK * (h + 1)], in0=z_ps[i][h][:], scalar1=1.0, scalar2=None,
+                op0=ALU.mult, op1=ALU.max, accum_out=half_best[i][h][:],
+            )
+
+        def join_best(i):
+            nc.vector.tensor_scalar(
+                out=minus_best[i][:], in0=half_best[i][0][:], scalar1=half_best[i][1][:], scalar2=-1.0, op0=ALU.max, op1=ALU.mult
+            )
+
+        def gather(i, j0, j1, picked):
+            nc.vector.tensor_copy(picked, z[i][:].indirect(offsets[:, j0 // 16 : j1 // 16]))
+
+        def exponential(i, j0, j1, picked):
+            nc.scalar.activation(out=decay[:, i, j0:j1], in_=picked, func=ACT.Exp, bias=minus_best[i][:])
+
+        def first_tile_piece(j0, j1, tag, align):
+            picked = keep.tile([P, j1 - j0], F32, name=f"picked0_{j0}", tag=tag, align_bytes=align)
+            gather(0, j0, j1, picked[:])
+            exponential(0, j0, j1, picked[:])
+            nc.scalar.activation(out=below[0][:, j0:j1], in_=picked[:], func=ACT.Identity, bias=minus_best[0][:])
+
+        for a in range(2):
+            round_x(0, a, VECTOR_COLS)
+            product_pass(0, a)
+        round_x(1, 0, 0)
+        round_x(1, 1, 0)
+        empty_bank(0, 0)
+        product_pass(1, 0)
+        empty_bank(0, 1)
+        product_pass(1, 1)
+        join_best(0)
+        first_tile_piece(0, 256, "x_raw11", None)
+        empty_bank(1, 0)
+        first_tile_piece(256, 384, "wc_last0", 64)
+        empty_bank(1, 1)
+        first_tile_piece(384, 512, "wc_last1", 64)
+        join_best(1)
+        picked = keep.tile([P, J], F32, name="picked1")
+        for j0, j1 in ((0, 320), (320, J)):
+            gather(1, j0, j1, picked[:, j0:j1])
+            exponential(1, j0, j1, picked[:, j0:j1])
+
+        s_ps = [psum.tile([P, J], F32, name=f"s_ps{i}", tag=f"bank1{i}") for i in range(2)]
+        for i in range(2):
             nc.tensor.matmul_mx(
                 out=s_ps[i][:],
                 lhsT=xs_w[:, 4 * P * i : 4 * P * (i + 1)].bitcast(FP8X4),
@@ -128,20 +155,16 @@ def tile_list_runner_up_gap_kernel(tc, xt, wc_words, wc_scales, xs_words, xs_sca
                 stop=True,
             )
 
-        gaps = []
-        both = keep.tile([P, TILES, J], F32, name="both", tag=f"z{TILES - 1}")
-        rest = keep.tile([P, TILES, J], F32, name="rest")
-        for i in range(TILES):
-            gap = both[:, i, :]
-            nc.vector.tensor_scalar(out=gap, in0=picked[i][:], scalar1=-1.0, scalar2=best[i][:], op0=ALU.mult, op1=ALU.add)
-            gaps.append(gap)
-        for i in range(TILES):
-            nc.vector.scalar_tensor_tensor(out=rest[:, i, :], in0=s_ps[i][:], scalar=-0.5, in1=gaps[i], op0=ALU.mult, op1=ALU.add)
+        nc.vector.tensor_scalar(out=below[1][:], in0=picked[:], scalar1=minus_best[1][:], scalar2=None, op0=ALU.add)
+        rest = keep.tile([P, 2, J], F32, name="rest", tag="z1")
+        for i in range(2):
+            nc.vector.scalar_tensor_tensor(out=rest[:, i, :], in0=s_ps[i][:], scalar=0.5, in1=below[i][:], op0=ALU.mult, op1=ALU.add)
 
         out_rows = out.rearrange("(i p) j -> p i j", p=P)
-        for j0, j1 in reversed(list(zip(OUT_CUTS[:-1], OUT_CUTS[1:]))):
-            soft = keep.tile([P, TILES, j1 - j0], F32, name=f"soft{j0}")
-            nc.scalar.activation(out=soft[:], in_=decay[:, :, j0:j1], func=ACT.Ln, bias=1.0)
-            y = keep.tile([P, TILES, j1 - j0], F32, name=f"y{j0}")
-            nc.vector.tensor_tensor(out=y[:], in0=rest[:, :, j0:j1], in1=soft[:], op=ALU.add)
-            nc.sync.dma_start(out=out_rows[:, :, j0:j1], in_=y[:])
+        for j0 in reversed(range(0, J, OUT_COLS)):
+            cols = slice(j0, j0 + OUT_COLS)
+            soft = keep.tile([P, 2, OUT_COLS], F32, name=f"soft{j0}")
+            nc.scalar.activation(out=soft[:], in_=decay[:, :, cols], func=ACT.Ln, bias=1.0)
+            y = keep.tile([P, 2, OUT_COLS], F32, name=f"y{j0}")
+            nc.vector.tensor_tensor(out=y[:], in0=soft[:], in1=rest[:, :, cols], op=ALU.subtract)
+            nc.sync.dma_start(out=out_rows[:, :, cols], in_=y[:])

@@ -20,7 +20,7 @@ P = 128
 PACK = 4
 BANK = 512
 VECTOR_COLS = 80
-OUT_COLS = 128
+OUT_COLS = 256
 
 
 def tile_list_runner_up_gap_kernel(tc, xt, wc_words, wc_scales, xs_words, xs_scales, ws_words, ws_scales, offs, out):
@@ -30,7 +30,9 @@ def tile_list_runner_up_gap_kernel(tc, xt, wc_words, wc_scales, xs_words, xs_sca
         psum = ctx.enter_context(tc.psum_pool(name="psum", bufs=1))
 
         offsets = keep.tile([P, J // 16], U16, name="offsets")
-        x_raw = [[keep.tile([P, PACK, P], F32, name=f"x_raw{i}{a}", tag=f"x_raw{i}{a}") for a in range(2)] for i in range(2)]
+        x_first = keep.tile([P, PACK, T], F32, name="x_first")
+        x_last = [keep.tile([P, PACK, P], F32, name=f"x_last{i}", tag=f"x_last{i}") for i in range(2)]
+        x_raw = [[x_first[:, :, i * P : (i + 1) * P], x_last[i][:]] for i in range(2)]
         wc_first = keep.tile([P, 2 * C], U8, name="wc_first", align_bytes=64)
         wc_last = [keep.tile([P, 2 * BANK], U8, name=f"wc_last{h}", tag=f"wc_last{h}", align_bytes=64) for h in range(2)]
         wc_s = keep.tile([P, 2 * C], U8, name="wc_s", align_bytes=64)
@@ -43,22 +45,18 @@ def tile_list_runner_up_gap_kernel(tc, xt, wc_words, wc_scales, xs_words, xs_sca
         nc.vector.memset(xs_s[:].bitcast(I32), 0)
         nc.vector.memset(ws_s[:].bitcast(I32), 0)
 
-        def load_x(i, a):
-            rows = xt[a * P * PACK : (a + 1) * P * PACK, i * P : (i + 1) * P]
-            nc.sync.dma_start(out=x_raw[i][a][:], in_=rows.rearrange("(p j) t -> p j t", j=PACK))
-
-        load_x(0, 0)
+        x_rows = xt.rearrange("(a p j) t -> a p j t", p=P, j=PACK)
+        nc.sync.dma_start(out=x_first[:], in_=x_rows[0])
         nc.sync.dma_start(out=wc_first[:].bitcast(I32), in_=wc_words[0].bitcast(I32))
         for q in range(4):
             nc.sync.dma_start(
                 out=wc_s[32 * q : 32 * q + 4, :].bitcast(I32).rearrange("r (z c) -> r z c", z=2),
                 in_=wc_scales.bitcast(I32)[:, 4 * q : 4 * q + 4, :].rearrange("z r c -> r z c"),
             )
-        load_x(0, 1)
+        nc.sync.dma_start(out=x_last[0][:], in_=x_rows[1][:, :, 0:P])
         for h in range(2):
             nc.sync.dma_start(out=wc_last[h][:].bitcast(I32), in_=wc_words[1].bitcast(I32)[:, h * BANK // 2 : (h + 1) * BANK // 2])
-        load_x(1, 0)
-        load_x(1, 1)
+        nc.sync.dma_start(out=x_last[1][:], in_=x_rows[1][:, :, P:T])
         nc.sync.dma_start(offsets[:], offs)
         nc.sync.dma_start(out=xs_w[:].bitcast(I32), in_=xs_words[0].rearrange("p t r -> p (t r)").bitcast(I32))
         nc.sync.dma_start(out=ws_w[:].bitcast(I32), in_=ws_words[0].bitcast(I32))
@@ -75,16 +73,16 @@ def tile_list_runner_up_gap_kernel(tc, xt, wc_words, wc_scales, xs_words, xs_sca
         x_bf = {}
 
         def round_x(i, a, vector_cols):
-            x_bf[i, a] = keep.tile([P, P, PACK], BF16, name=f"x_bf{i}{a}", align_bytes=64)
-            src = x_raw[i][a][:].rearrange("p j (c e) -> p c j e", e=4)
+            x_bf[i, a] = keep.tile([P, P, PACK], BF16, name=f"x_bf{i}{a}", tag=f"x_bf{i}{a}", align_bytes=64)
+            src = x_raw[i][a].rearrange("p j (c e) -> p c j e", e=4)
             dst = x_bf[i, a][:].rearrange("p (c e) j -> p c j e", e=4)
             cut = vector_cols // 4
             if cut > 0:
                 nc.vector.tensor_copy(out=dst[:, :cut], in_=src[:, :cut])
             nc.scalar.copy(out=dst[:, cut:], in_=src[:, cut:])
 
-        def product_pass(i, a):
-            x_q = keep.tile([P, P], U32, name=f"x_q{i}{a}", align_bytes=64)
+        def product_pass(i, a, tag):
+            x_q = keep.tile([P, P], U32, name=f"x_q{i}{a}", tag=tag, align_bytes=64)
             x_s = keep.tile([P, P], U8, name=f"x_s{i}{a}", align_bytes=64)
             nc.vector.quantize_mx(out=x_q[:].bitcast(FP8X4), scales=x_s[:], in_=x_bf[i, a][:].rearrange("p c j -> p (c j)"))
             for h in range(2):
@@ -122,23 +120,24 @@ def tile_list_runner_up_gap_kernel(tc, xt, wc_words, wc_scales, xs_words, xs_sca
             exponential(0, j0, j1, picked[:])
             nc.scalar.activation(out=below[0][:, j0:j1], in_=picked[:], func=ACT.Identity, bias=minus_best[0][:])
 
-        for a in range(2):
-            round_x(0, a, VECTOR_COLS)
-            product_pass(0, a)
+        round_x(0, 0, VECTOR_COLS)
+        product_pass(0, 0, "x_q00")
         round_x(1, 0, 0)
+        round_x(0, 1, VECTOR_COLS)
+        product_pass(0, 1, "x_q01")
+        product_pass(1, 0, "x_bf01")
         round_x(1, 1, 0)
         empty_bank(0, 0)
-        product_pass(1, 0)
         empty_bank(0, 1)
-        product_pass(1, 1)
+        product_pass(1, 1, "x_q11")
         join_best(0)
-        first_tile_piece(0, 256, "x_raw11", None)
+        first_tile_piece(0, 256, "x_last1", None)
         empty_bank(1, 0)
         first_tile_piece(256, 384, "wc_last0", 64)
         empty_bank(1, 1)
         first_tile_piece(384, 512, "wc_last1", 64)
         join_best(1)
-        picked = keep.tile([P, J], F32, name="picked1")
+        picked = keep.tile([P, J], F32, name="picked1", tag="picked1")
         for j0, j1 in ((0, 320), (320, J)):
             gather(1, j0, j1, picked[:, j0:j1])
             exponential(1, j0, j1, picked[:, j0:j1])
@@ -155,16 +154,17 @@ def tile_list_runner_up_gap_kernel(tc, xt, wc_words, wc_scales, xs_words, xs_sca
                 stop=True,
             )
 
-        nc.vector.tensor_scalar(out=below[1][:], in0=picked[:], scalar1=minus_best[1][:], scalar2=None, op0=ALU.add)
         rest = keep.tile([P, 2, J], F32, name="rest", tag="z1")
         for i in range(2):
+            if i == 1:
+                nc.vector.tensor_scalar(out=below[1][:], in0=picked[:], scalar1=minus_best[1][:], scalar2=None, op0=ALU.add)
             nc.vector.scalar_tensor_tensor(out=rest[:, i, :], in0=s_ps[i][:], scalar=0.5, in1=below[i][:], op0=ALU.mult, op1=ALU.add)
 
-        out_rows = out.rearrange("(i p) j -> p i j", p=P)
-        for j0 in reversed(range(0, J, OUT_COLS)):
-            cols = slice(j0, j0 + OUT_COLS)
-            soft = keep.tile([P, 2, OUT_COLS], F32, name=f"soft{j0}")
-            nc.scalar.activation(out=soft[:], in_=decay[:, :, cols], func=ACT.Ln, bias=1.0)
-            y = keep.tile([P, 2, OUT_COLS], F32, name=f"y{j0}")
-            nc.vector.tensor_tensor(out=y[:], in0=soft[:], in1=rest[:, :, cols], op=ALU.subtract)
-            nc.sync.dma_start(out=out_rows[:, :, cols], in_=y[:])
+        soft = [keep.tile([P, J], F32, name="soft0", tag="picked1"), keep.tile([P, J], F32, name="soft1")]
+        for i in range(2):
+            for j0 in range(0, J, OUT_COLS):
+                cols = slice(j0, j0 + OUT_COLS)
+                nc.scalar.activation(out=soft[i][:, cols], in_=decay[:, i, cols], func=ACT.Ln, bias=1.0)
+                y = keep.tile([P, OUT_COLS], F32, name=f"y{i}_{j0}")
+                nc.vector.tensor_tensor(out=y[:], in0=soft[i][:, cols], in1=rest[:, i, cols], op=ALU.subtract)
+                nc.sync.dma_start(out=out[i * P : (i + 1) * P, cols], in_=y[:])

@@ -20,7 +20,7 @@ P = 128
 PACK = 4
 BANK = 512
 VECTOR_COLS = 80
-OUT_COLS = 256
+OUT_CUTS = ((0, 128, 320, J), (0, 192, 384, J))
 
 
 def tile_list_runner_up_gap_kernel(tc, xt, wc_words, wc_scales, xs_words, xs_scales, ws_words, ws_scales, offs, out):
@@ -30,11 +30,8 @@ def tile_list_runner_up_gap_kernel(tc, xt, wc_words, wc_scales, xs_words, xs_sca
         psum = ctx.enter_context(tc.psum_pool(name="psum", bufs=1))
 
         offsets = keep.tile([P, J // 16], U16, name="offsets")
-        x_first = keep.tile([P, PACK, T], F32, name="x_first")
-        x_last = [keep.tile([P, PACK, P], F32, name=f"x_last{i}", tag=f"x_last{i}") for i in range(2)]
-        x_raw = [[x_first[:, :, i * P : (i + 1) * P], x_last[i][:]] for i in range(2)]
-        wc_first = keep.tile([P, 2 * C], U8, name="wc_first", align_bytes=64)
-        wc_last = [keep.tile([P, 2 * BANK], U8, name=f"wc_last{h}", tag=f"wc_last{h}", align_bytes=64) for h in range(2)]
+        x_raw = [[keep.tile([P, PACK, P], F32, name=f"x_raw{i}{a}", tag=f"x_raw{i}{a}") for a in range(2)] for i in range(2)]
+        wc_w = [keep.tile([P, 4 * BANK], U8, name=f"wc_w{h}", tag=f"wc_w{h}", align_bytes=64) for h in range(2)]
         wc_s = keep.tile([P, 2 * C], U8, name="wc_s", align_bytes=64)
         xs_w = keep.tile([P, 4 * T], U8, name="xs_w", align_bytes=64)
         ws_w = keep.tile([P, 2 * J], U8, name="ws_w", align_bytes=64)
@@ -46,23 +43,26 @@ def tile_list_runner_up_gap_kernel(tc, xt, wc_words, wc_scales, xs_words, xs_sca
         nc.vector.memset(ws_s[:].bitcast(I32), 0)
 
         x_rows = xt.rearrange("(a p j) t -> a p j t", p=P, j=PACK)
-        nc.sync.dma_start(out=x_first[:], in_=x_rows[0])
-        nc.sync.dma_start(out=wc_first[:].bitcast(I32), in_=wc_words[0].bitcast(I32))
+        for a in range(2):
+            nc.sync.dma_start(out=x_raw[0][a][:], in_=x_rows[a][:, :, 0:P])
         for q in range(4):
             nc.sync.dma_start(
-                out=wc_s[32 * q : 32 * q + 4, :].bitcast(I32).rearrange("r (z c) -> r z c", z=2),
-                in_=wc_scales.bitcast(I32)[:, 4 * q : 4 * q + 4, :].rearrange("z r c -> r z c"),
+                out=wc_s[q:P:32, :].bitcast(I32).rearrange("q (z c) -> q z c", z=2),
+                in_=wc_scales.bitcast(I32)[:, q:16:4, :].rearrange("z q c -> q z c"),
             )
-        nc.sync.dma_start(out=x_last[0][:], in_=x_rows[1][:, :, 0:P])
         for h in range(2):
-            nc.sync.dma_start(out=wc_last[h][:].bitcast(I32), in_=wc_words[1].bitcast(I32)[:, h * BANK // 2 : (h + 1) * BANK // 2])
-        nc.sync.dma_start(out=x_last[1][:], in_=x_rows[1][:, :, P:T])
+            nc.sync.dma_start(
+                out=wc_w[h][:].bitcast(I32).rearrange("p (z c) -> p z c", z=2),
+                in_=wc_words.bitcast(I32)[:, :, h * BANK // 2 : (h + 1) * BANK // 2].rearrange("z p c -> p z c"),
+            )
+        for a in range(2):
+            nc.sync.dma_start(out=x_raw[1][a][:], in_=x_rows[a][:, :, P:T])
         nc.sync.dma_start(offsets[:], offs)
         nc.sync.dma_start(out=xs_w[:].bitcast(I32), in_=xs_words[0].rearrange("p t r -> p (t r)").bitcast(I32))
         nc.sync.dma_start(out=ws_w[:].bitcast(I32), in_=ws_words[0].bitcast(I32))
         for q in range(4):
-            nc.sync.dma_start(out=xs_s[32 * q : 32 * q + 4, :].bitcast(I32), in_=xs_scales[0].bitcast(I32)[4 * q : 4 * q + 4, :])
-            nc.sync.dma_start(out=ws_s[32 * q : 32 * q + 4, :].bitcast(I32), in_=ws_scales[0].bitcast(I32)[4 * q : 4 * q + 4, :])
+            nc.sync.dma_start(out=xs_s[q:P:32, :].bitcast(I32), in_=xs_scales[0].bitcast(I32)[q:16:4, :])
+            nc.sync.dma_start(out=ws_s[q:P:32, :].bitcast(I32), in_=ws_scales[0].bitcast(I32)[q:16:4, :])
 
         z_ps = [[psum.tile([P, BANK], F32, name=f"z_ps{i}{h}", tag=f"bank{i}{h}") for h in range(2)] for i in range(2)]
         z = [keep.tile([P, C], F32, name=f"z{i}", tag=f"z{i}") for i in range(2)]
@@ -71,31 +71,36 @@ def tile_list_runner_up_gap_kernel(tc, xt, wc_words, wc_scales, xs_words, xs_sca
         decay = keep.tile([P, 2, J], F32, name="decay")
         below = [keep.tile([P, J], F32, name=f"below{i}") for i in range(2)]
         x_bf = {}
+        x_mx = {}
 
         def round_x(i, a, vector_cols):
             x_bf[i, a] = keep.tile([P, P, PACK], BF16, name=f"x_bf{i}{a}", tag=f"x_bf{i}{a}", align_bytes=64)
-            src = x_raw[i][a].rearrange("p j (c e) -> p c j e", e=4)
+            src = x_raw[i][a][:].rearrange("p j (c e) -> p c j e", e=4)
             dst = x_bf[i, a][:].rearrange("p (c e) j -> p c j e", e=4)
             cut = vector_cols // 4
             if cut > 0:
                 nc.vector.tensor_copy(out=dst[:, :cut], in_=src[:, :cut])
             nc.scalar.copy(out=dst[:, cut:], in_=src[:, cut:])
 
-        def product_pass(i, a, tag):
-            x_q = keep.tile([P, P], U32, name=f"x_q{i}{a}", tag=tag, align_bytes=64)
+        def quantise(i, a):
+            x_q = keep.tile([P, P], U32, name=f"x_q{i}{a}", align_bytes=64)
             x_s = keep.tile([P, P], U8, name=f"x_s{i}{a}", align_bytes=64)
             nc.vector.quantize_mx(out=x_q[:].bitcast(FP8X4), scales=x_s[:], in_=x_bf[i, a][:].rearrange("p c j -> p (c j)"))
+            x_mx[i, a] = (x_q, x_s)
+
+        def product(i):
             for h in range(2):
-                words = wc_first[:, 2 * BANK * h : 2 * BANK * (h + 1)] if a == 0 else wc_last[h][:]
-                nc.tensor.matmul_mx(
-                    out=z_ps[i][h][:],
-                    lhsT=x_q[:].bitcast(FP8X4),
-                    lhsT_scale=x_s[:],
-                    rhs=words.bitcast(FP4X4),
-                    rhs_scale=wc_s[:, a * C + BANK * h : a * C + BANK * (h + 1)],
-                    start=(a == 0),
-                    stop=(a == 1),
-                )
+                for a in range(2):
+                    x_q, x_s = x_mx[i, a]
+                    nc.tensor.matmul_mx(
+                        out=z_ps[i][h][:],
+                        lhsT=x_q[:].bitcast(FP8X4),
+                        lhsT_scale=x_s[:],
+                        rhs=wc_w[h][:, 2 * BANK * a : 2 * BANK * (a + 1)].bitcast(FP4X4),
+                        rhs_scale=wc_s[:, a * C + BANK * h : a * C + BANK * (h + 1)],
+                        start=(a == 0),
+                        stop=(a == 1),
+                    )
 
         def empty_bank(i, h):
             nc.vector.tensor_scalar(
@@ -120,22 +125,22 @@ def tile_list_runner_up_gap_kernel(tc, xt, wc_words, wc_scales, xs_words, xs_sca
             exponential(0, j0, j1, picked[:])
             nc.scalar.activation(out=below[0][:, j0:j1], in_=picked[:], func=ACT.Identity, bias=minus_best[0][:])
 
-        round_x(0, 0, VECTOR_COLS)
-        product_pass(0, 0, "x_q00")
+        for a in range(2):
+            round_x(0, a, VECTOR_COLS)
+            quantise(0, a)
+        product(0)
         round_x(1, 0, 0)
-        round_x(0, 1, VECTOR_COLS)
-        product_pass(0, 1, "x_q01")
-        product_pass(1, 0, "x_bf01")
         round_x(1, 1, 0)
         empty_bank(0, 0)
+        quantise(1, 0)
         empty_bank(0, 1)
-        product_pass(1, 1, "x_q11")
+        quantise(1, 1)
+        product(1)
         join_best(0)
-        first_tile_piece(0, 256, "x_last1", None)
+        first_tile_piece(0, 384, "x_raw11", None)
         empty_bank(1, 0)
-        first_tile_piece(256, 384, "wc_last0", 64)
         empty_bank(1, 1)
-        first_tile_piece(384, 512, "wc_last1", 64)
+        first_tile_piece(384, 512, "wc_w1", 64)
         join_best(1)
         picked = keep.tile([P, J], F32, name="picked1", tag="picked1")
         for j0, j1 in ((0, 320), (320, J)):
@@ -162,9 +167,9 @@ def tile_list_runner_up_gap_kernel(tc, xt, wc_words, wc_scales, xs_words, xs_sca
 
         soft = [keep.tile([P, J], F32, name="soft0", tag="picked1"), keep.tile([P, J], F32, name="soft1")]
         for i in range(2):
-            for j0 in range(0, J, OUT_COLS):
-                cols = slice(j0, j0 + OUT_COLS)
+            for j0, j1 in zip(OUT_CUTS[i][:-1], OUT_CUTS[i][1:]):
+                cols = slice(j0, j1)
                 nc.scalar.activation(out=soft[i][:, cols], in_=decay[:, i, cols], func=ACT.Ln, bias=1.0)
-                y = keep.tile([P, OUT_COLS], F32, name=f"y{i}_{j0}")
+                y = keep.tile([P, j1 - j0], F32, name=f"y{i}_{j0}")
                 nc.vector.tensor_tensor(out=y[:], in0=soft[i][:, cols], in1=rest[:, i, cols], op=ALU.subtract)
                 nc.sync.dma_start(out=out[i * P : (i + 1) * P, cols], in_=y[:])

@@ -19,7 +19,17 @@ ACT = mybir.ActivationFunctionType
 P = 128
 PACK = 4
 BANK = 512
-VECTOR_COLS = 80
+PASSES = K // (P * PACK)
+TILES = T // P
+HALVES = C // BANK
+BLOCKS = 16
+QUADRANT = 32
+LIST_ROWS = 16
+LINE = 4
+
+VECTOR_TOKENS = 80
+FIRST_CUT = 384
+SECOND_CUT = 320
 OUT_CUTS = ((0, 128, 320, J), (0, 192, 384, J))
 
 
@@ -29,10 +39,13 @@ def tile_list_runner_up_gap_kernel(tc, xt, wc_words, wc_scales, xs_words, xs_sca
         keep = ctx.enter_context(tc.tile_pool(name="keep", bufs=1))
         psum = ctx.enter_context(tc.psum_pool(name="psum", bufs=1))
 
-        offsets = keep.tile([P, J // 16], U16, name="offsets")
-        x_raw = [[keep.tile([P, PACK, P], F32, name=f"x_raw{i}{a}", tag=f"x_raw{i}{a}") for a in range(2)] for i in range(2)]
-        wc_w = [keep.tile([P, 4 * BANK], U8, name=f"wc_w{h}", tag=f"wc_w{h}", align_bytes=64) for h in range(2)]
-        wc_s = keep.tile([P, 2 * C], U8, name="wc_s", align_bytes=64)
+        offsets = keep.tile([P, J // LIST_ROWS], U16, name="offsets")
+        x_raw = [
+            [keep.tile([P, PACK, P], F32, name=f"x_raw{i}{a}", tag=f"x_raw{i}{a}") for a in range(PASSES)]
+            for i in range(TILES)
+        ]
+        wc_w = [keep.tile([P, 2 * C], U8, name=f"wc_w{a}", tag=f"wc_w{a}", align_bytes=64) for a in range(PASSES)]
+        wc_s = keep.tile([P, PASSES * C], U8, name="wc_s", align_bytes=64)
         xs_w = keep.tile([P, 4 * T], U8, name="xs_w", align_bytes=64)
         ws_w = keep.tile([P, 2 * J], U8, name="ws_w", align_bytes=64)
         xs_s = keep.tile([P, T], U8, name="xs_s", align_bytes=64)
@@ -42,42 +55,42 @@ def tile_list_runner_up_gap_kernel(tc, xt, wc_words, wc_scales, xs_words, xs_sca
         nc.vector.memset(xs_s[:].bitcast(I32), 0)
         nc.vector.memset(ws_s[:].bitcast(I32), 0)
 
-        x_rows = xt.rearrange("(a p j) t -> a p j t", p=P, j=PACK)
-        for a in range(2):
-            nc.sync.dma_start(out=x_raw[0][a][:], in_=x_rows[a][:, :, 0:P])
-        for q in range(4):
+        x_rows = xt.rearrange("(a p r) t -> a p r t", p=P, r=PACK)
+        nc.sync.dma_start(out=x_raw[0][0][:], in_=x_rows[0][:, :, 0:P])
+        nc.sync.dma_start(out=wc_w[0][:].bitcast(I32), in_=wc_words[0].bitcast(I32))
+        for r in range(4):
             nc.sync.dma_start(
-                out=wc_s[q:P:32, :].bitcast(I32).rearrange("q (z c) -> q z c", z=2),
-                in_=wc_scales.bitcast(I32)[:, q:16:4, :].rearrange("z q c -> q z c"),
+                out=wc_s[r:P:QUADRANT, :].bitcast(I32).rearrange("q (a c) -> q a c", a=PASSES),
+                in_=wc_scales.bitcast(I32)[:, r:BLOCKS:4, :].rearrange("a q c -> q a c"),
             )
-        for h in range(2):
-            nc.sync.dma_start(
-                out=wc_w[h][:].bitcast(I32).rearrange("p (z c) -> p z c", z=2),
-                in_=wc_words.bitcast(I32)[:, :, h * BANK // 2 : (h + 1) * BANK // 2].rearrange("z p c -> p z c"),
-            )
-        for a in range(2):
+        nc.sync.dma_start(out=x_raw[0][1][:], in_=x_rows[1][:, :, 0:P])
+        nc.sync.dma_start(out=wc_w[1][:].bitcast(I32), in_=wc_words[1].bitcast(I32))
+        for a in range(PASSES):
             nc.sync.dma_start(out=x_raw[1][a][:], in_=x_rows[a][:, :, P:T])
         nc.sync.dma_start(offsets[:], offs)
         nc.sync.dma_start(out=xs_w[:].bitcast(I32), in_=xs_words[0].rearrange("p t r -> p (t r)").bitcast(I32))
         nc.sync.dma_start(out=ws_w[:].bitcast(I32), in_=ws_words[0].bitcast(I32))
-        for q in range(4):
-            nc.sync.dma_start(out=xs_s[q:P:32, :].bitcast(I32), in_=xs_scales[0].bitcast(I32)[q:16:4, :])
-            nc.sync.dma_start(out=ws_s[q:P:32, :].bitcast(I32), in_=ws_scales[0].bitcast(I32)[q:16:4, :])
+        for r in range(4):
+            nc.sync.dma_start(out=xs_s[r:P:QUADRANT, :].bitcast(I32), in_=xs_scales[0].bitcast(I32)[r:BLOCKS:4, :])
+            nc.sync.dma_start(out=ws_s[r:P:QUADRANT, :].bitcast(I32), in_=ws_scales[0].bitcast(I32)[r:BLOCKS:4, :])
 
-        z_ps = [[psum.tile([P, BANK], F32, name=f"z_ps{i}{h}", tag=f"bank{i}{h}") for h in range(2)] for i in range(2)]
-        z = [keep.tile([P, C], F32, name=f"z{i}", tag=f"z{i}") for i in range(2)]
-        half_best = [[keep.tile([P, 1], F32, name=f"half_best{i}{h}") for h in range(2)] for i in range(2)]
-        minus_best = [keep.tile([P, 1], F32, name=f"minus_best{i}") for i in range(2)]
-        decay = keep.tile([P, 2, J], F32, name="decay")
-        below = [keep.tile([P, J], F32, name=f"below{i}") for i in range(2)]
+        z_ps = [
+            [psum.tile([P, BANK], F32, name=f"z_ps{i}{h}", tag=f"bank{i}{h}") for h in range(HALVES)]
+            for i in range(TILES)
+        ]
+        z = [keep.tile([P, C], F32, name=f"z{i}", tag=f"z{i}") for i in range(TILES)]
+        half_best = [[keep.tile([P, 1], F32, name=f"half_best{i}{h}") for h in range(HALVES)] for i in range(TILES)]
+        minus_best = [keep.tile([P, 1], F32, name=f"minus_best{i}") for i in range(TILES)]
+        decay = keep.tile([P, TILES, J], F32, name="decay")
+        below = [keep.tile([P, J], F32, name=f"below{i}") for i in range(TILES)]
         x_bf = {}
         x_mx = {}
 
-        def round_x(i, a, vector_cols):
+        def round_x(i, a, vector_tokens):
             x_bf[i, a] = keep.tile([P, P, PACK], BF16, name=f"x_bf{i}{a}", tag=f"x_bf{i}{a}", align_bytes=64)
-            src = x_raw[i][a][:].rearrange("p j (c e) -> p c j e", e=4)
-            dst = x_bf[i, a][:].rearrange("p (c e) j -> p c j e", e=4)
-            cut = vector_cols // 4
+            src = x_raw[i][a][:].rearrange("p r (g e) -> p g r e", e=LINE)
+            dst = x_bf[i, a][:].rearrange("p (g e) r -> p g r e", e=LINE)
+            cut = vector_tokens // LINE
             if cut > 0:
                 nc.vector.tensor_copy(out=dst[:, :cut], in_=src[:, :cut])
             nc.scalar.copy(out=dst[:, cut:], in_=src[:, cut:])
@@ -85,70 +98,78 @@ def tile_list_runner_up_gap_kernel(tc, xt, wc_words, wc_scales, xs_words, xs_sca
         def quantise(i, a):
             x_q = keep.tile([P, P], U32, name=f"x_q{i}{a}", align_bytes=64)
             x_s = keep.tile([P, P], U8, name=f"x_s{i}{a}", align_bytes=64)
-            nc.vector.quantize_mx(out=x_q[:].bitcast(FP8X4), scales=x_s[:], in_=x_bf[i, a][:].rearrange("p c j -> p (c j)"))
+            nc.vector.quantize_mx(out=x_q[:].bitcast(FP8X4), scales=x_s[:], in_=x_bf[i, a][:].rearrange("p t r -> p (t r)"))
             x_mx[i, a] = (x_q, x_s)
 
-        def product(i):
-            for h in range(2):
-                for a in range(2):
+        def scores(i):
+            for a in range(PASSES):
+                for h in range(HALVES):
                     x_q, x_s = x_mx[i, a]
                     nc.tensor.matmul_mx(
                         out=z_ps[i][h][:],
                         lhsT=x_q[:].bitcast(FP8X4),
                         lhsT_scale=x_s[:],
-                        rhs=wc_w[h][:, 2 * BANK * a : 2 * BANK * (a + 1)].bitcast(FP4X4),
+                        rhs=wc_w[a][:, 2 * BANK * h : 2 * BANK * (h + 1)].bitcast(FP4X4),
                         rhs_scale=wc_s[:, a * C + BANK * h : a * C + BANK * (h + 1)],
                         start=(a == 0),
-                        stop=(a == 1),
+                        stop=(a == PASSES - 1),
                     )
 
         def empty_bank(i, h):
             nc.vector.tensor_scalar(
-                out=z[i][:, BANK * h : BANK * (h + 1)], in0=z_ps[i][h][:], scalar1=1.0, scalar2=None,
-                op0=ALU.mult, op1=ALU.max, accum_out=half_best[i][h][:],
+                out=z[i][:, BANK * h : BANK * (h + 1)],
+                in0=z_ps[i][h][:],
+                scalar1=1.0,
+                scalar2=None,
+                op0=ALU.mult,
+                op1=ALU.max,
+                accum_out=half_best[i][h][:],
             )
 
         def join_best(i):
             nc.vector.tensor_scalar(
-                out=minus_best[i][:], in0=half_best[i][0][:], scalar1=half_best[i][1][:], scalar2=-1.0, op0=ALU.max, op1=ALU.mult
+                out=minus_best[i][:],
+                in0=half_best[i][0][:],
+                scalar1=half_best[i][1][:],
+                scalar2=-1.0,
+                op0=ALU.max,
+                op1=ALU.mult,
             )
 
-        def gather(i, j0, j1, picked):
-            nc.vector.tensor_copy(picked, z[i][:].indirect(offsets[:, j0 // 16 : j1 // 16]))
-
-        def exponential(i, j0, j1, picked):
+        def gather_and_exp(i, j0, j1, picked):
+            nc.vector.tensor_copy(picked, z[i][:].indirect(offsets[:, j0 // LIST_ROWS : j1 // LIST_ROWS]))
             nc.scalar.activation(out=decay[:, i, j0:j1], in_=picked, func=ACT.Exp, bias=minus_best[i][:])
 
         def first_tile_piece(j0, j1, tag, align):
             picked = keep.tile([P, j1 - j0], F32, name=f"picked0_{j0}", tag=tag, align_bytes=align)
-            gather(0, j0, j1, picked[:])
-            exponential(0, j0, j1, picked[:])
+            gather_and_exp(0, j0, j1, picked[:])
             nc.scalar.activation(out=below[0][:, j0:j1], in_=picked[:], func=ACT.Identity, bias=minus_best[0][:])
 
-        for a in range(2):
-            round_x(0, a, VECTOR_COLS)
+        for a in range(PASSES):
+            round_x(0, a, VECTOR_TOKENS)
             quantise(0, a)
-        product(0)
+        scores(0)
+
         round_x(1, 0, 0)
         round_x(1, 1, 0)
         empty_bank(0, 0)
         quantise(1, 0)
         empty_bank(0, 1)
         quantise(1, 1)
-        product(1)
+        scores(1)
         join_best(0)
-        first_tile_piece(0, 384, "x_raw11", None)
+
+        first_tile_piece(0, FIRST_CUT, "x_raw11", None)
         empty_bank(1, 0)
         empty_bank(1, 1)
-        first_tile_piece(384, 512, "wc_w1", 64)
+        first_tile_piece(FIRST_CUT, J, "wc_w1", 64)
         join_best(1)
-        picked = keep.tile([P, J], F32, name="picked1", tag="picked1")
-        for j0, j1 in ((0, 320), (320, J)):
-            gather(1, j0, j1, picked[:, j0:j1])
-            exponential(1, j0, j1, picked[:, j0:j1])
+        picked_last = keep.tile([P, J], F32, name="picked_last", tag="picked_last")
+        for j0, j1 in ((0, SECOND_CUT), (SECOND_CUT, J)):
+            gather_and_exp(1, j0, j1, picked_last[:, j0:j1])
 
-        s_ps = [psum.tile([P, J], F32, name=f"s_ps{i}", tag=f"bank1{i}") for i in range(2)]
-        for i in range(2):
+        s_ps = [psum.tile([P, J], F32, name=f"s_ps{i}", tag=f"bank1{i}") for i in range(TILES)]
+        for i in range(TILES):
             nc.tensor.matmul_mx(
                 out=s_ps[i][:],
                 lhsT=xs_w[:, 4 * P * i : 4 * P * (i + 1)].bitcast(FP8X4),
@@ -159,14 +180,19 @@ def tile_list_runner_up_gap_kernel(tc, xt, wc_words, wc_scales, xs_words, xs_sca
                 stop=True,
             )
 
-        rest = keep.tile([P, 2, J], F32, name="rest", tag="z1")
-        for i in range(2):
-            if i == 1:
-                nc.vector.tensor_scalar(out=below[1][:], in0=picked[:], scalar1=minus_best[1][:], scalar2=None, op0=ALU.add)
-            nc.vector.scalar_tensor_tensor(out=rest[:, i, :], in0=s_ps[i][:], scalar=0.5, in1=below[i][:], op0=ALU.mult, op1=ALU.add)
+        rest = keep.tile([P, TILES, J], F32, name="rest", tag="z1")
 
-        soft = [keep.tile([P, J], F32, name="soft0", tag="picked1"), keep.tile([P, J], F32, name="soft1")]
-        for i in range(2):
+        def add_half_s(i):
+            nc.vector.scalar_tensor_tensor(
+                out=rest[:, i, :], in0=s_ps[i][:], scalar=0.5, in1=below[i][:], op0=ALU.mult, op1=ALU.add
+            )
+
+        add_half_s(0)
+        nc.vector.tensor_scalar(out=below[1][:], in0=picked_last[:], scalar1=minus_best[1][:], scalar2=None, op0=ALU.add)
+        add_half_s(1)
+
+        soft = [keep.tile([P, J], F32, name="soft0", tag="picked_last"), keep.tile([P, J], F32, name="soft1")]
+        for i in range(TILES):
             for j0, j1 in zip(OUT_CUTS[i][:-1], OUT_CUTS[i][1:]):
                 cols = slice(j0, j1)
                 nc.scalar.activation(out=soft[i][:, cols], in_=decay[:, i, cols], func=ACT.Ln, bias=1.0)

from contextlib import ExitStack

import concourse.mybir as mybir

K, L, T, C, J = 1024, 512, 256, 1024, 512
FLOPS = 2 * K * T * C + 2 * L * T * J

F32 = mybir.dt.float32
BF16 = mybir.dt.bfloat16
I32 = mybir.dt.int32
U32 = mybir.dt.uint32
U16 = mybir.dt.uint16
U8 = mybir.dt.uint8
FP8X4 = mybir.dt.float8_e4m3fn_x4
FP4X4 = mybir.dt.float4_e2m1fn_x4
ALU = mybir.AluOpType
ACT = mybir.ActivationFunctionType

P = 128
PACK = 4
BANK = 512
PASSES = K // (P * PACK)
TILES = T // P
HALVES = C // BANK
BLOCKS = 16
QUADRANT = 32
LIST_ROWS = 16
LINE = 4

VECTOR_TOKENS = 80
FIRST_CUT = 384
SECOND_CUT = 320
OUT_CUTS = ((0, 128, 320, J), (0, 192, 384, J))


def tile_list_runner_up_gap_kernel(tc, xt, wc_words, wc_scales, xs_words, xs_scales, ws_words, ws_scales, offs, out):
    nc = tc.nc
    with ExitStack() as ctx:
        keep = ctx.enter_context(tc.tile_pool(name="keep", bufs=1))
        psum = ctx.enter_context(tc.psum_pool(name="psum", bufs=1))

        offsets = keep.tile([P, J // LIST_ROWS], U16, name="offsets")
        x_raw = [
            [keep.tile([P, PACK, P], F32, name=f"x_raw{i}{a}", tag=f"x_raw{i}{a}") for a in range(PASSES)]
            for i in range(TILES)
        ]
        wc_w = [keep.tile([P, 2 * C], U8, name=f"wc_w{a}", tag=f"wc_w{a}", align_bytes=64) for a in range(PASSES)]
        wc_s = keep.tile([P, PASSES * C], U8, name="wc_s", align_bytes=64)
        xs_w = keep.tile([P, 4 * T], U8, name="xs_w", align_bytes=64)
        ws_w = keep.tile([P, 2 * J], U8, name="ws_w", align_bytes=64)
        xs_s = keep.tile([P, T], U8, name="xs_s", align_bytes=64)
        ws_s = keep.tile([P, J], U8, name="ws_s", align_bytes=64)

        nc.vector.memset(wc_s[:].bitcast(I32), 0)
        nc.vector.memset(xs_s[:].bitcast(I32), 0)
        nc.vector.memset(ws_s[:].bitcast(I32), 0)

        x_rows = xt.rearrange("(a p r) t -> a p r t", p=P, r=PACK)
        nc.sync.dma_start(out=x_raw[0][0][:], in_=x_rows[0][:, :, 0:P])
        nc.sync.dma_start(out=wc_w[0][:].bitcast(I32), in_=wc_words[0].bitcast(I32))
        for r in range(4):
            nc.sync.dma_start(
                out=wc_s[r:P:QUADRANT, :].bitcast(I32).rearrange("q (a c) -> q a c", a=PASSES),
                in_=wc_scales.bitcast(I32)[:, r:BLOCKS:4, :].rearrange("a q c -> q a c"),
            )
        nc.sync.dma_start(out=x_raw[0][1][:], in_=x_rows[1][:, :, 0:P])
        nc.sync.dma_start(out=wc_w[1][:].bitcast(I32), in_=wc_words[1].bitcast(I32))
        for a in range(PASSES):
            nc.sync.dma_start(out=x_raw[1][a][:], in_=x_rows[a][:, :, P:T])
        nc.sync.dma_start(offsets[:], offs)
        nc.sync.dma_start(out=xs_w[:].bitcast(I32), in_=xs_words[0].rearrange("p t r -> p (t r)").bitcast(I32))
        nc.sync.dma_start(out=ws_w[:].bitcast(I32), in_=ws_words[0].bitcast(I32))
        for r in range(4):
            nc.sync.dma_start(out=xs_s[r:P:QUADRANT, :].bitcast(I32), in_=xs_scales[0].bitcast(I32)[r:BLOCKS:4, :])
            nc.sync.dma_start(out=ws_s[r:P:QUADRANT, :].bitcast(I32), in_=ws_scales[0].bitcast(I32)[r:BLOCKS:4, :])

        z_ps = [
            [psum.tile([P, BANK], F32, name=f"z_ps{i}{h}", tag=f"bank{i}{h}") for h in range(HALVES)]
            for i in range(TILES)
        ]
        z = [keep.tile([P, C], F32, name=f"z{i}", tag=f"z{i}") for i in range(TILES)]
        half_best = [[keep.tile([P, 1], F32, name=f"half_best{i}{h}") for h in range(HALVES)] for i in range(TILES)]
        minus_best = [keep.tile([P, 1], F32, name=f"minus_best{i}") for i in range(TILES)]
        decay = keep.tile([P, TILES, J], F32, name="decay")
        below = [keep.tile([P, J], F32, name=f"below{i}") for i in range(TILES)]
        x_bf = {}
        x_mx = {}

        def round_x(i, a, vector_tokens):
            x_bf[i, a] = keep.tile([P, P, PACK], BF16, name=f"x_bf{i}{a}", tag=f"x_bf{i}{a}", align_bytes=64)
            src = x_raw[i][a][:].rearrange("p r (g e) -> p g r e", e=LINE)
            dst = x_bf[i, a][:].rearrange("p (g e) r -> p g r e", e=LINE)
            cut = vector_tokens // LINE
            if cut > 0:
                nc.vector.tensor_copy(out=dst[:, :cut], in_=src[:, :cut])
            nc.scalar.copy(out=dst[:, cut:], in_=src[:, cut:])

        def quantise(i, a):
            x_q = keep.tile([P, P], U32, name=f"x_q{i}{a}", align_bytes=64)
            x_s = keep.tile([P, P], U8, name=f"x_s{i}{a}", align_bytes=64)
            nc.vector.quantize_mx(out=x_q[:].bitcast(FP8X4), scales=x_s[:], in_=x_bf[i, a][:].rearrange("p t r -> p (t r)"))
            x_mx[i, a] = (x_q, x_s)

        def scores(i):
            for a in range(PASSES):
                for h in range(HALVES):
                    x_q, x_s = x_mx[i, a]
                    nc.tensor.matmul_mx(
                        out=z_ps[i][h][:],
                        lhsT=x_q[:].bitcast(FP8X4),
                        lhsT_scale=x_s[:],
                        rhs=wc_w[a][:, 2 * BANK * h : 2 * BANK * (h + 1)].bitcast(FP4X4),
                        rhs_scale=wc_s[:, a * C + BANK * h : a * C + BANK * (h + 1)],
                        start=(a == 0),
                        stop=(a == PASSES - 1),
                    )

        def empty_bank(i, h):
            nc.vector.tensor_scalar(
                out=z[i][:, BANK * h : BANK * (h + 1)],
                in0=z_ps[i][h][:],
                scalar1=1.0,
                scalar2=None,
                op0=ALU.mult,
                op1=ALU.max,
                accum_out=half_best[i][h][:],
            )

        def join_best(i):
            nc.vector.tensor_scalar(
                out=minus_best[i][:],
                in0=half_best[i][0][:],
                scalar1=half_best[i][1][:],
                scalar2=-1.0,
                op0=ALU.max,
                op1=ALU.mult,
            )

        def gather_and_exp(i, j0, j1, picked):
            nc.vector.tensor_copy(picked, z[i][:].indirect(offsets[:, j0 // LIST_ROWS : j1 // LIST_ROWS]))
            nc.scalar.activation(out=decay[:, i, j0:j1], in_=picked, func=ACT.Exp, bias=minus_best[i][:])

        def first_tile_piece(j0, j1, tag, align):
            picked = keep.tile([P, j1 - j0], F32, name=f"picked0_{j0}", tag=tag, align_bytes=align)
            gather_and_exp(0, j0, j1, picked[:])
            nc.scalar.activation(out=below[0][:, j0:j1], in_=picked[:], func=ACT.Identity, bias=minus_best[0][:])

        for a in range(PASSES):
            round_x(0, a, VECTOR_TOKENS)
            quantise(0, a)
        scores(0)

        round_x(1, 0, 0)
        round_x(1, 1, 0)
        empty_bank(0, 0)
        quantise(1, 0)
        empty_bank(0, 1)
        quantise(1, 1)
        scores(1)
        join_best(0)

        first_tile_piece(0, FIRST_CUT, "x_raw11", None)
        empty_bank(1, 0)
        empty_bank(1, 1)
        first_tile_piece(FIRST_CUT, J, "wc_w1", 64)
        join_best(1)
        picked_last = keep.tile([P, J], F32, name="picked_last", tag="picked_last")
        for j0, j1 in ((0, SECOND_CUT), (SECOND_CUT, J)):
            gather_and_exp(1, j0, j1, picked_last[:, j0:j1])

        s_ps = [psum.tile([P, J], F32, name=f"s_ps{i}", tag=f"bank1{i}") for i in range(TILES)]
        for i in range(TILES):
            nc.tensor.matmul_mx(
                out=s_ps[i][:],
                lhsT=xs_w[:, 4 * P * i : 4 * P * (i + 1)].bitcast(FP8X4),
                lhsT_scale=xs_s[:, P * i : P * (i + 1)],
                rhs=ws_w[:].bitcast(FP4X4),
                rhs_scale=ws_s[:],
                start=True,
                stop=True,
            )

        rest = keep.tile([P, TILES, J], F32, name="rest", tag="z1")

        def add_half_s(i):
            nc.vector.scalar_tensor_tensor(
                out=rest[:, i, :], in0=s_ps[i][:], scalar=0.5, in1=below[i][:], op0=ALU.mult, op1=ALU.add
            )

        add_half_s(0)
        nc.vector.tensor_scalar(out=below[1][:], in0=picked_last[:], scalar1=minus_best[1][:], scalar2=None, op0=ALU.add)
        add_half_s(1)

        soft = [keep.tile([P, J], F32, name="soft0", tag="picked_last"), keep.tile([P, J], F32, name="soft1")]
        for i in range(TILES):
            for j0, j1 in zip(OUT_CUTS[i][:-1], OUT_CUTS[i][1:]):
                cols = slice(j0, j1)
                nc.scalar.activation(out=soft[i][:, cols], in_=decay[:, i, cols], func=ACT.Ln, bias=1.0)
                y = keep.tile([P, j1 - j0], F32, name=f"y{i}_{j0}")
                nc.vector.tensor_tensor(out=y[:], in0=soft[i][:, cols], in1=rest[:, i, cols], op=ALU.subtract)
                nc.sync.dma_start(out=out[i * P : (i + 1) * P, cols], in_=y[:])
